import numpy as np
import ml_dtypes

BF16 = ml_dtypes.bfloat16


def bf(x):
    return np.asarray(x, np.float32).astype(BF16)


def f32(x):
    return np.asarray(x, np.float32)


def f64(x):
    return np.asarray(x).astype(np.float64)


def striped(idx):
    return np.tile(idx.reshape(-1, 16).T, (8, 1))


S, K, M, N, D, V = 512, 128, 256, 768, 8, 96


def setup_inputs():
    return {"table": bf(np.random.standard_normal((S, K))), "w": bf(np.random.standard_normal((K, M)) / np.sqrt(D * K)), "c": f32(0.2 + 0.8 * np.random.random_sample((1, V))), "offs": striped(np.random.permutation(np.tile(np.arange(S), 2))[:N])}


def reference(table, w, c, offs):
    idx = offs[:16].T.reshape(-1)
    x = f64(table)[idx].T
    y = f64(w).T @ sum(x[:, t * V : (t + 1) * V] for t in range(D))
    return y * f64(c)

@@ -1,0 +1,57 @@
+import concourse.mybir as mybir
+from concourse.masks import make_identity
+
+BF16, F32, U16 = mybir.dt.bfloat16, mybir.dt.float32, mybir.dt.uint16
+
+P = 128
+NODES, K, M = 512, 128, 256
+NEIGHBOURS, V = 8, 96
+N = NEIGHBOURS * V
+PIECE_COLUMNS = V // 16
+HALVES = 2
+HALF_BLOCKS = NODES // P // HALVES
+
+FLOPS = 2 * K * M * N
+
+
+def tile_gather_matmul_kernel(tc, table, w, c, offs, out):
+    nc = tc.nc
+    with (
+        tc.tile_pool(name="held", bufs=1) as held,
+        tc.psum_pool(name="flip", bufs=HALVES) as flip,
+        tc.psum_pool(name="sums", bufs=M // P) as sums,
+    ):
+        rows = held.tile([P, NODES // P, K], BF16)
+        nc.sync.dma_start(rows[:], table.rearrange("(b p) k -> p b k", p=P))
+        offsets = held.tile([P, N // 16], U16)
+        nc.sync.dma_start(offsets[:], offs)
+        weights = held.tile([P, M], BF16)
+        nc.scalar.dma_start(weights[:], w)
+        node_weight = held.tile([P, V], F32)
+        nc.scalar.dma_start(node_weight[:], c.rearrange("o v -> (o v)").partition_broadcast(P))
+
+        identity = held.tile([P, P], BF16)
+        make_identity(nc, identity[:])
+
+        nodes = held.tile([P, NODES], BF16)
+        half_width = HALF_BLOCKS * P
+        for h in range(HALVES):
+            flipped = flip.tile([P, half_width], BF16)
+            for i in range(HALF_BLOCKS):
+                nc.tensor.transpose(flipped[:, i * P : (i + 1) * P], rows[:, h * HALF_BLOCKS + i, :], identity[:])
+            nc.vector.tensor_copy(nodes[:, h * half_width : (h + 1) * half_width], flipped[:])
+
+        for m in range(M // P):
+            summed = sums.tile([P, V], F32)
+            for t in range(NEIGHBOURS):
+                piece = offsets[:, t * PIECE_COLUMNS : (t + 1) * PIECE_COLUMNS]
+                nc.tensor.matmul(
+                    summed[:],
+                    weights[:, m * P : (m + 1) * P],
+                    nodes[:].indirect(piece),
+                    start=(t == 0),
+                    stop=(t == NEIGHBOURS - 1),
+                )
+            result = held.tile([P, V], F32, name=f"result{m}")
+            nc.vector.tensor_tensor(result[:], summed[:], node_weight[:], mybir.AluOpType.mult)
+            nc.sync.dma_start(out[m * P : (m + 1) * P, :], result[:])

@@ -26,9 +26,9 @@ def tile_gather_matmul_kernel(tc, table, w, c, offs, out):
         offsets = held.tile([P, N // 16], U16)
         nc.sync.dma_start(offsets[:], offs)
         weights = held.tile([P, M], BF16)
-        nc.scalar.dma_start(weights[:], w)
+        nc.sync.dma_start(weights[:], w)
         node_weight = held.tile([P, V], F32)
-        nc.scalar.dma_start(node_weight[:], c.rearrange("o v -> (o v)").partition_broadcast(P))
+        nc.sync.dma_start(node_weight[:], c.rearrange("o v -> (o v)").partition_broadcast(P))
 
         identity = held.tile([P, P], BF16)
         make_identity(nc, identity[:])

@@ -10,6 +10,8 @@ N = NEIGHBOURS * V
 PIECE_COLUMNS = V // 16
 HALVES = 2
 HALF_BLOCKS = NODES // P // HALVES
+WARM_COLUMNS = 512
+WARM_MATMULS = 4
 
 FLOPS = 2 * K * M * N
 
@@ -17,6 +19,7 @@ FLOPS = 2 * K * M * N
 def tile_gather_matmul_kernel(tc, table, w, c, offs, out):
     nc = tc.nc
     with (
+        tc.psum_pool(name="warm", bufs=1) as warm,
         tc.tile_pool(name="held", bufs=1) as held,
         tc.psum_pool(name="flip", bufs=HALVES) as flip,
         tc.psum_pool(name="sums", bufs=M // P) as sums,
@@ -29,6 +32,12 @@ def tile_gather_matmul_kernel(tc, table, w, c, offs, out):
         nc.sync.dma_start(weights[:], w)
         node_weight = held.tile([P, V], F32)
         nc.sync.dma_start(node_weight[:], c.rearrange("o v -> (o v)").partition_broadcast(P))
+
+        zeros = held.tile([P, WARM_COLUMNS], BF16)
+        nc.vector.memset(zeros[:], 0.0)
+        unread = warm.tile([P, WARM_COLUMNS], F32)
+        for i in range(WARM_MATMULS):
+            nc.tensor.matmul(unread[:], zeros[:, :P], zeros[:], start=True, stop=True)
 
         identity = held.tile([P, P], BF16)
         make_identity(nc, identity[:])

import concourse.mybir as mybir
from concourse.masks import make_identity

BF16, F32, U16 = mybir.dt.bfloat16, mybir.dt.float32, mybir.dt.uint16

P = 128
NODES, K, M = 512, 128, 256
NEIGHBOURS, V = 8, 96
N = NEIGHBOURS * V
PIECE_COLUMNS = V // 16
HALVES = 2
HALF_BLOCKS = NODES // P // HALVES
WARM_COLUMNS = 512
WARM_MATMULS = 4

FLOPS = 2 * K * M * N


def tile_gather_matmul_kernel(tc, table, w, c, offs, out):
    nc = tc.nc
    with (
        tc.psum_pool(name="warm", bufs=1) as warm,
        tc.tile_pool(name="held", bufs=1) as held,
        tc.psum_pool(name="flip", bufs=HALVES) as flip,
        tc.psum_pool(name="sums", bufs=M // P) as sums,
    ):
        rows = held.tile([P, NODES // P, K], BF16)
        nc.sync.dma_start(rows[:], table.rearrange("(b p) k -> p b k", p=P))
        offsets = held.tile([P, N // 16], U16)
        nc.sync.dma_start(offsets[:], offs)
        weights = held.tile([P, M], BF16)
        nc.sync.dma_start(weights[:], w)
        node_weight = held.tile([P, V], F32)
        nc.sync.dma_start(node_weight[:], c.rearrange("o v -> (o v)").partition_broadcast(P))

        zeros = held.tile([P, WARM_COLUMNS], BF16)
        nc.vector.memset(zeros[:], 0.0)
        unread = warm.tile([P, WARM_COLUMNS], F32)
        for i in range(WARM_MATMULS):
            nc.tensor.matmul(unread[:], zeros[:, :P], zeros[:], start=True, stop=True)

        identity = held.tile([P, P], BF16)
        make_identity(nc, identity[:])

        nodes = held.tile([P, NODES], BF16)
        half_width = HALF_BLOCKS * P
        for h in range(HALVES):
            flipped = flip.tile([P, half_width], BF16)
            for i in range(HALF_BLOCKS):
                nc.tensor.transpose(flipped[:, i * P : (i + 1) * P], rows[:, h * HALF_BLOCKS + i, :], identity[:])
            nc.vector.tensor_copy(nodes[:, h * half_width : (h + 1) * half_width], flipped[:])

        for m in range(M // P):
            summed = sums.tile([P, V], F32)
            for t in range(NEIGHBOURS):
                piece = offsets[:, t * PIECE_COLUMNS : (t + 1) * PIECE_COLUMNS]
                nc.tensor.matmul(
                    summed[:],
                    weights[:, m * P : (m + 1) * P],
                    nodes[:].indirect(piece),
                    start=(t == 0),
                    stop=(t == NEIGHBOURS - 1),
                )
            result = held.tile([P, V], F32, name=f"result{m}")
            nc.vector.tensor_tensor(result[:], summed[:], node_weight[:], mybir.AluOpType.mult)
            nc.sync.dma_start(out[m * P : (m + 1) * P, :], result[:])
